import numpy as np
import ml_dtypes


def mxq(x, axis, fmt="e4m3"):
    dtype, down = {"e4m3": (ml_dtypes.float8_e4m3fn, 7), "e5m2": (ml_dtypes.float8_e5m2, 14)}[fmt]
    v = np.moveaxis(np.asarray(x, np.float32).astype(ml_dtypes.bfloat16).astype(np.float64), axis, -1)
    blocks = v.reshape(v.shape[:-1] + (-1, 32))
    amax = np.abs(blocks).max(-1, keepdims=True)
    byte = np.maximum(np.where(amax > 0, np.frexp(amax)[1] - 1 + 127, 0) - down, 1)
    scale = np.exp2(byte - 127.0)
    codes = (blocks / scale).astype(np.float32).astype(dtype).astype(np.float64)
    return np.moveaxis((codes * scale).reshape(v.shape), -1, axis)


WIDE = False


def mx_kscale(k):
    if not WIDE:
        return np.ones(k)
    levels = np.array([10, -10, 5, -5, 0])
    if k % 512:
        return np.exp2(np.random.permutation(np.resize(levels, k // 32))).repeat(32)
    a = np.empty((k // 512, 16))
    for p in range(k // 512):
        a[p, :8] = np.random.permutation(np.resize(levels, 8))
        for g in range(8):
            far = levels[np.abs(levels - a[p, g]) >= 10]
            a[p, g + 8] = far[np.random.randint(len(far))]
    return np.exp2(a.ravel()).repeat(32)


def f64(x):
    return np.asarray(x).astype(np.float64)


def striped(idx):
    return np.tile(idx.reshape(-1, 16).T, (8, 1)).astype(np.uint16)


def unstriped(offs):
    return offs[:16].T.reshape(-1).astype(np.int64)


def striped8(idx):
    return np.concatenate([x.reshape(-1, 16).T for x in idx]).astype(np.uint16)


def runs(offs, k):
    lists = np.stack([offs[16 * r : 16 * r + 16].T.reshape(-1) for r in range(8)]).astype(np.int64)
    return lists[np.arange(k) % 512 // 64]


def pack_weight(w):
    k, n = w.shape
    w = f64(np.asarray(w, np.float32).astype(ml_dtypes.bfloat16)).reshape(k // 32, 32, n)
    amax = np.abs(w).max(1)
    byte = np.clip(np.where(amax > 0, np.frexp(amax)[1] - 1 + 127 - 7, 1), 1, 254)
    scaled = (w * np.exp2(127.0 - byte)[:, None, :]).reshape(k, n).astype(np.float32)
    words = np.ascontiguousarray(scaled.reshape(k // 512, 128, 4, n).transpose(0, 1, 3, 2)).astype(ml_dtypes.float8_e4m3fn).view(np.uint8)
    return words, np.ascontiguousarray(byte.astype(np.uint8).reshape(k // 512, 16, n))


def unpack_weight(words, scales):
    g, p, n, _ = words.shape
    vals = np.ascontiguousarray(words).view(ml_dtypes.float8_e4m3fn).astype(np.float64) * np.repeat(np.exp2(scales.astype(np.float64) - 127.0), 8, axis=1)[..., None]
    return vals.transpose(0, 1, 3, 2).reshape(g * 512, n)


K, T, S, N, H, W, C = 512, 2048, 512, 512, 512, 256, 512


def setup_inputs():
    n = np.random.standard_normal
    s = mx_kscale(K)[:, None]
    u = mx_kscale(S)
    packed_xT = pack_weight(n((K, T)) * s)
    perm = np.stack([np.random.permutation(S) for _ in range(8)])
    return {
        "x_words": packed_xT[0],
        "x_scales": packed_xT[1],
        "w1": (n((K, H)) / np.sqrt(K) / s).astype(np.float32),
        "gn": (np.random.uniform(0.5, 1.5, (H, 1)) * u[:, None]).astype(np.float32),
        "w2": (n((H, N)) / np.sqrt(H) / u[:, None]).astype(np.float32),
        "gs": (np.random.uniform(0.5, 1.5, (K, 1)) / s).astype(np.float32),
        "offs": striped(np.random.permutation(T)[:S]),
        "n1": striped8(np.stack([np.random.permutation(S) for _ in range(8)])),
        "n2": striped8(perm[:, :W]),
        "n3": striped8(perm[:, W:]),
        "cand": striped(np.random.permutation(T)[:C]),
        "n4": striped8(np.stack([np.random.permutation(S)[:W] for _ in range(8)])),
        "n5": striped8(np.stack([np.random.permutation(S)[:W] for _ in range(8)])),
    }


def reference(x_words, x_scales, w1, gn, w2, gs, offs, n1, n2, n3, cand, n4, n5):
    x_cand = unpack_weight(x_words, x_scales)[:, unstriped(cand)]
    xq = unpack_weight(x_words, x_scales)[:, unstriped(offs)]
    y = mxq(f64(w1), 0, "e4m3").T @ xq
    pa = y[np.arange(H)[:, None], runs(n2, H)]
    pb = y[np.arange(H)[:, None], runs(n3, H)]
    rb = np.maximum(0.5 * pa, pb)
    ra = pb - pa
    ds = np.zeros((H, S))
    ds[np.arange(H)[:, None], runs(n2, H)] = ra
    dt = ds.copy()
    dt[np.arange(H)[:, None], runs(n3, H)] = rb
    z2 = f64(gs) * dt
    b = 0.0625 * ((x_cand.T @ mxq(z2, 0, "e4m3")))
    z = f64(gn) * (np.maximum(y, y[np.arange(H)[:, None], runs(n1, H)]))
    a = mxq(f64(w2), 0, "e4m3").T @ mxq(z, 0, "e4m3")
    ra2 = b[np.arange(C)[:, None], runs(n5, C)] - (0.5 * (a[np.arange(N)[:, None], runs(n4, N)]))
    out = a.copy()
    out[np.arange(C)[:, None], runs(n4, C)] = ra2
    return out

@@ -1,0 +1,222 @@
+from contextlib import ExitStack
+
+import concourse.mybir as mybir
+
+F32 = mybir.dt.float32
+BF16 = mybir.dt.bfloat16
+I32 = mybir.dt.int32
+U32 = mybir.dt.uint32
+U16 = mybir.dt.uint16
+U8 = mybir.dt.uint8
+FP8X4 = mybir.dt.float8_e4m3fn_x4
+ALU = mybir.AluOpType
+COPY = mybir.ActivationFunctionType.Copy
+
+P = 128
+PACK = 4
+T = 2048
+S = 512
+W = 256
+FLOPS = 3 * 2 * 512 * 512 * 512
+
+
+def tile_picked_fkcdputbbiglift_none_p_kernel(tc, x_words, x_scales, w1, gn, w2, gs, offs, n1, n2, n3, cand, n4, n5, out):
+    nc = tc.nc
+    with ExitStack() as ctx:
+        keep = ctx.enter_context(tc.tile_pool(name="keep", bufs=1))
+        psum = ctx.enter_context(tc.psum_pool(name="psum", bufs=1))
+
+        def sb(name, shape, dtype):
+            return keep.tile(shape, dtype, name=name, align_bytes=64)
+
+        def load_list(name, src):
+            tile = sb(name, list(src.shape), U16)
+            nc.sync.dma_start(out=tile[:], in_=src)
+            return tile
+
+
+        xs = sb("xs", [P, T], U8)
+        nc.vector.memset(xs[:].bitcast(I32), 0)
+        gn_t = sb("gn_t", [P, PACK], F32)
+        gs_t = sb("gs_t", [P, PACK], F32)
+        w1_rows = w1.rearrange("(p j) c -> p j c", j=PACK)
+        w2_rows = w2.rearrange("(p j) c -> p j c", j=PACK)
+        offs_t = load_list("offs_t", offs)
+        w1_raw = [sb(f"w1_raw{h}", [P, PACK, W], F32) for h in range(2)]
+        nc.sync.dma_start(out=w1_raw[0][:], in_=w1_rows[:, :, 0:W])
+        for q in range(4):
+            nc.sync.dma_start(out=xs[32 * q : 32 * q + 4, :].bitcast(I32), in_=x_scales[0, 4 * q : 4 * q + 4, :].bitcast(I32))
+        cand_t = load_list("cand_t", cand)
+        nc.sync.dma_start(out=w1_raw[1][:], in_=w1_rows[:, :, W:S])
+        xw = sb("xw", [P, T], I32)
+        nc.sync.dma_start(out=xw[:], in_=x_words[0].rearrange("p n r -> p (n r)").bitcast(I32))
+        n2_t = load_list("n2_t", n2)
+        n3_t = load_list("n3_t", n3)
+        n1_t = load_list("n1_t", n1)
+        nc.sync.dma_start(out=gn_t[:], in_=gn.rearrange("(p t) o -> p (t o)", t=PACK))
+        w2_raw = sb("w2_raw", [P, PACK, S], F32)
+        nc.sync.dma_start(out=w2_raw[:], in_=w2_rows)
+        nc.sync.dma_start(out=gs_t[:], in_=gs.rearrange("(p t) o -> p (t o)", t=PACK))
+        n4_t = load_list("n4_t", n4)
+        n5_t = load_list("n5_t", n5)
+
+        def deal_weight(dst, raw, m0, m1):
+            nc.scalar.copy(
+                out=dst[:].rearrange("p (t m j) -> p m j t", t=PACK, j=PACK)[:, m0:m1],
+                in_=raw.rearrange("p j (m t) -> p m j t", t=PACK),
+            )
+
+        def quantize(name, src):
+            codes = sb(name + "_c", [P, S], U32)
+            scales = sb(name + "_s", [P, S], U8)
+            nc.vector.quantize_mx(out=codes[:].bitcast(FP8X4), scales=scales[:], in_=src[:])
+            return codes, scales
+
+        def product(bank, t, left, right):
+            cols = slice(P * t, P * (t + 1))
+            nc.tensor.matmul_mx(out=bank[:], lhsT=left[0][:, cols].bitcast(FP8X4), lhsT_scale=left[1][:, cols],
+                                rhs=right[0][:].bitcast(FP8X4), rhs_scale=right[1][:], start=True, stop=True)
+
+        def interleave(name, planes):
+            dst = sb(name, [P, PACK * S], BF16)
+            nc.vector.tensor_copy(
+                out=dst[:].rearrange("p (c i t) -> p c t i", i=4, t=PACK),
+                in_=planes[:].rearrange("p t (c i) -> p c t i", i=4),
+            )
+            return dst
+
+
+        def product_half(bank, t, h, left, right):
+            cols = slice(P * t, P * (t + 1))
+            half = slice(W * h, W * (h + 1))
+            nc.tensor.matmul_mx(out=bank[:, half], lhsT=left[0][:, cols].bitcast(FP8X4), lhsT_scale=left[1][:, cols],
+                                rhs=right[0][:, half].bitcast(FP8X4), rhs_scale=right[1][:, half], start=True, stop=True)
+
+        def gather(eng, dst, window, lst, scale=1.0):
+            if eng == "S":
+                nc.scalar.activation(dst, window.indirect(lst), COPY, scale=scale)
+            elif scale == 1.0:
+                nc.vector.tensor_copy(dst, window.indirect(lst))
+            else:
+                nc.vector.tensor_scalar(dst, window.indirect(lst), scale, 0.0, ALU.mult, ALU.add)
+
+        def cast(eng, dst, src, col):
+            if eng == "S":
+                nc.scalar.activation(dst, src, COPY, scale=col)
+            elif eng == "G":
+                nc.gpsimd.tensor_scalar(dst, src, col, 0.0, ALU.mult, ALU.add)
+            else:
+                nc.vector.tensor_scalar(dst, src, col, None, ALU.mult)
+
+        w1_g = sb("w1_g", [P, PACK * S], BF16)
+        deal_weight(w1_g, w1_raw[0][:], 0, 64)
+        deal_weight(w1_g, w1_raw[1][:], 64, 128)
+
+        xq_s = sb("xq_s", [P, S], U8)
+        nc.vector.tensor_copy(out=xq_s[:], in_=xs[:].indirect(offs_t[:]))
+        xc_s0 = sb("xc_s0", [P, S], U8)
+        nc.vector.tensor_copy(out=xc_s0[:], in_=xs[:].indirect(cand_t[:]))
+        xc_s = sb("xc_s", [P, S], U8)
+        nc.vector.tensor_copy(out=xc_s[:].rearrange("p (t m) -> p m t", t=PACK), in_=xc_s0[:].rearrange("p (m t) -> p m t", t=PACK))
+        w1_q = quantize("w1", w1_g)
+        xq_w = sb("xq_w", [P, S], U32)
+        banks_y = [psum.tile([P, S], F32, name=f"bank_y{t}", tag=f"yb{t}") for t in range(PACK)]
+        y = [sb(f"y{t}", [P, S], F32) for t in range(PACK)]
+        for h in range(2):
+            half = slice(W * h, W * (h + 1))
+            nc.vector.tensor_copy(out=xq_w[:, half], in_=xw[:].bitcast(U32).indirect(offs_t[:, 16 * h : 16 * (h + 1)]))
+            product_half(banks_y[0], 0, h, w1_q, (xq_w, xq_s))
+            nc.scalar.copy(out=y[0][:, half], in_=banks_y[0][:, half])
+        for t in range(1, PACK):
+            product(banks_y[t], t, w1_q, (xq_w, xq_s))
+
+        xc_w0 = sb("xc_w0", [P, S], U32)
+        nc.vector.tensor_copy(out=xc_w0[:], in_=xw[:].bitcast(U32).indirect(cand_t[:]))
+        xc_w = sb("xc_w", [P, S], U32)
+        nc.vector.tensor_copy(out=xc_w[:].bitcast(I32).rearrange("p (t m) -> p m t", t=PACK), in_=xc_w0[:].bitcast(I32).rearrange("p (m t) -> p m t", t=PACK))
+
+        z_planes = sb("z_planes", [P, PACK, S], BF16)
+        z2_planes = sb("z2_planes", [P, PACK, S], BF16)
+        w2_g = sb("w2_g", [P, PACK * S], BF16)
+        dt = [sb(f"dt{t}", [P, S], F32) for t in range(PACK)]
+        big = [sb(f"big{t}", [P, S], F32) for t in range(PACK)]
+
+        def evac_y(t):
+            nc.scalar.copy(out=y[t][:], in_=banks_y[t][:])
+
+        def pairs(t, eng_b="S"):
+            npa = sb(f"npa{t}", [P, W], F32)
+            pb = sb(f"pb{t}", [P, W], F32)
+            gather("S", npa[:], y[t][:], n2_t[:], -1.0)
+            gather(eng_b, pb[:], y[t][:], n3_t[:])
+            nc.vector.tensor_tensor(dt[t][:].indirect(n2_t[:]), pb[:], npa[:], ALU.add)
+            rb = sb(f"rb{t}", [P, W], F32)
+            nc.vector.scalar_tensor_tensor(rb[:], npa[:], -0.5, pb[:], ALU.mult, ALU.max)
+            nc.vector.tensor_copy(dt[t][:].indirect(n3_t[:]), rb[:])
+
+        def neigh(t):
+            g1 = sb(f"g1{t}", [P, S], F32)
+            for h in range(2):
+                gather("S", g1[:, W * h : W * (h + 1)], y[t][:], n1_t[:, 16 * h : 16 * (h + 1)])
+            nc.vector.tensor_tensor(big[t][:], g1[:], y[t][:], ALU.max)
+
+        def cz(t, eng):
+            cast(eng, z_planes[:, t, :], big[t][:], gn_t[:, t : t + 1])
+
+        def cd(t, eng):
+            cast(eng, z2_planes[:, t, :], dt[t][:], gs_t[:, t : t + 1])
+
+        pairs(0, "V")
+        evac_y(1)
+        neigh(0)
+        pairs(1)
+        evac_y(2)
+        neigh(1)
+        evac_y(3)
+        neigh(2)
+        pairs(2)
+        neigh(3)
+        cz(3, "V")
+        cz(0, "S")
+        cz(1, "S")
+        cz(2, "S")
+        z_q = quantize("z", interleave("z_g", z_planes))
+        for h in range(2):
+            deal_weight(w2_g, w2_raw[:, :, W * h : W * (h + 1)], 64 * h, 64 * (h + 1))
+        w2_q = quantize("w2", w2_g)
+        banks_a = [psum.tile([P, S], F32, name=f"bank_a{t}", tag=f"ab{t}") for t in range(PACK)]
+        for t in range(PACK):
+            product(banks_a[t], t, w2_q, z_q)
+        pairs(3)
+        cd(3, "V")
+        for t in range(3):
+            cd(t, "S")
+        z2_g = interleave("z2_g", z2_planes)
+        z2_c = sb("z2_c", [P, S], U32)
+        z2_s = sb("z2_s", [P, S], U8)
+        for h in range(2):
+            half = slice(W * h, W * (h + 1))
+            nc.vector.quantize_mx(out=z2_c[:, half].bitcast(FP8X4), scales=z2_s[:, half], in_=z2_g[:, 4 * W * h : 4 * W * (h + 1)])
+        a = [sb(f"a{t}", [P, S], F32) for t in range(PACK)]
+        ga = [sb(f"ga{t}", [P, W], F32) for t in range(PACK)]
+        for t in range(PACK):
+            nc.scalar.copy(out=a[t][:], in_=banks_a[t][:])
+        for t in range(PACK):
+            gather("S" if t < 2 else "V", ga[t][:], a[t][:], n4_t[:], -0.5)
+
+        out_rows = out.rearrange("(p t) n -> p t n", t=PACK)
+        banks_b = [psum.tile([P, S], F32, name=f"bank_b{t}", tag=f"yb{t}") for t in range(PACK)]
+        b = [sb(f"b{t}", [P, S], F32) for t in range(PACK)]
+        for h in range(2):
+            half = slice(W * h, W * (h + 1))
+            product_half(banks_b[0], 0, h, (xc_w, xc_s), (z2_c, z2_s))
+            nc.scalar.copy(out=b[0][:, half], in_=banks_b[0][:, half])
+        for t in range(1, PACK):
+            product(banks_b[t], t, (xc_w, xc_s), (z2_c, z2_s))
+        for t in range(PACK):
+            if t > 0:
+                nc.scalar.copy(out=b[t][:], in_=banks_b[t][:])
+            gb = sb(f"gb{t}", [P, W], F32)
+            gather("S", gb[:], b[t][:], n5_t[:], 0.0625)
+            nc.vector.tensor_tensor(a[t][:].indirect(n4_t[:]), gb[:], ga[t][:], ALU.add)
+            nc.sync.dma_start(out=out_rows[:, t, :], in_=a[t][:])

@@ -52,10 +52,11 @@ def tile_picked_fkcdputbbiglift_none_p_kernel(tc, x_words, x_scales, w1, gn, w2,
         nc.sync.dma_start(out=xw[:], in_=x_words[0].rearrange("p n r -> p (n r)").bitcast(I32))
         n2_t = load_list("n2_t", n2)
         n3_t = load_list("n3_t", n3)
+        w2_raw = [sb(f"w2_raw{h}", [P, PACK, W], F32) for h in range(2)]
+        for h in range(2):
+            nc.sync.dma_start(out=w2_raw[h][:], in_=w2_rows[:, :, W * h : W * (h + 1)])
         n1_t = load_list("n1_t", n1)
         nc.sync.dma_start(out=gn_t[:], in_=gn.rearrange("(p t) o -> p (t o)", t=PACK))
-        w2_raw = sb("w2_raw", [P, PACK, S], F32)
-        nc.sync.dma_start(out=w2_raw[:], in_=w2_rows)
         nc.sync.dma_start(out=gs_t[:], in_=gs.rearrange("(p t) o -> p (t o)", t=PACK))
         n4_t = load_list("n4_t", n4)
         n5_t = load_list("n5_t", n5)
@@ -119,16 +120,23 @@ def tile_picked_fkcdputbbiglift_none_p_kernel(tc, x_words, x_scales, w1, gn, w2,
         xc_s = sb("xc_s", [P, S], U8)
         nc.vector.tensor_copy(out=xc_s[:].rearrange("p (t m) -> p m t", t=PACK), in_=xc_s0[:].rearrange("p (m t) -> p m t", t=PACK))
         w1_q = quantize("w1", w1_g)
-        xq_w = sb("xq_w", [P, S], U32)
-        banks_y = [psum.tile([P, S], F32, name=f"bank_y{t}", tag=f"yb{t}") for t in range(PACK)]
+        xq_w = [sb(f"xq_w{h}", [P, W], U32) for h in range(2)]
         y = [sb(f"y{t}", [P, S], F32) for t in range(PACK)]
+
+        def pass_half(bank, t, h, left, codes, scales):
+            cols = slice(P * t, P * (t + 1))
+            nc.tensor.matmul_mx(out=bank[:, W * h : W * (h + 1)], lhsT=left[0][:, cols].bitcast(FP8X4), lhsT_scale=left[1][:, cols],
+                                rhs=codes.bitcast(FP8X4), rhs_scale=scales, start=True, stop=True)
+
+        def y_pass(bank, t, h):
+            pass_half(bank, t, h, w1_q, xq_w[h][:], xq_s[:, W * h : W * (h + 1)])
+
         for h in range(2):
             half = slice(W * h, W * (h + 1))
-            nc.vector.tensor_copy(out=xq_w[:, half], in_=xw[:].bitcast(U32).indirect(offs_t[:, 16 * h : 16 * (h + 1)]))
-            product_half(banks_y[0], 0, h, w1_q, (xq_w, xq_s))
-            nc.scalar.copy(out=y[0][:, half], in_=banks_y[0][:, half])
-        for t in range(1, PACK):
-            product(banks_y[t], t, w1_q, (xq_w, xq_s))
+            nc.vector.tensor_copy(out=xq_w[h][:], in_=xw[:].bitcast(U32).indirect(offs_t[:, 16 * h : 16 * (h + 1)]))
+            bank = psum.tile([P, S], F32, name=f"bank_y0{h}", tag=f"yb{h}")
+            y_pass(bank, 0, h)
+            nc.scalar.copy(out=y[0][:, half], in_=bank[:, half])
 
         xc_w0 = sb("xc_w0", [P, S], U32)
         nc.vector.tensor_copy(out=xc_w0[:], in_=xw[:].bitcast(U32).indirect(cand_t[:]))
@@ -142,23 +150,107 @@ def tile_picked_fkcdputbbiglift_none_p_kernel(tc, x_words, x_scales, w1, gn, w2,
         big = [sb(f"big{t}", [P, S], F32) for t in range(PACK)]
 
         def evac_y(t):
-            nc.scalar.copy(out=y[t][:], in_=banks_y[t][:])
+            bank = psum.tile([P, S], F32, name=f"bank_y{t}", tag="yb1")
+            y_pass(bank, t, 0)
+            y_pass(bank, t, 1)
+            nc.scalar.copy(out=y[t][:], in_=bank[:])
 
-        def pairs(t, eng_b="S"):
-            npa = sb(f"npa{t}", [P, W], F32)
-            pb = sb(f"pb{t}", [P, W], F32)
-            gather("S", npa[:], y[t][:], n2_t[:], -1.0)
-            gather(eng_b, pb[:], y[t][:], n3_t[:])
-            nc.vector.tensor_tensor(dt[t][:].indirect(n2_t[:]), pb[:], npa[:], ALU.add)
-            rb = sb(f"rb{t}", [P, W], F32)
-            nc.vector.scalar_tensor_tensor(rb[:], npa[:], -0.5, pb[:], ALU.mult, ALU.max)
-            nc.vector.tensor_copy(dt[t][:].indirect(n3_t[:]), rb[:])
+        npa = [sb(f"npa{t}", [P, W], F32) for t in range(PACK)]
+        pb = [sb(f"pb{t}", [P, W], F32) for t in range(PACK)]
+        rb = [sb(f"rb{t}", [P, W], F32) for t in range(PACK)]
+        g1 = [sb(f"g1{t}", [P, S], F32) for t in range(PACK)]
+        a = [sb(f"a{t}", [P, S], F32) for t in range(PACK)]
+        b = [sb(f"b{t}", [P, S], F32) for t in range(PACK)]
+        ga = [sb(f"ga{t}", [P, W], F32) for t in range(PACK)]
+        gb = [sb(f"gb{t}", [P, W], F32) for t in range(PACK)]
+        z_g = sb("z_g", [P, PACK * S], BF16)
+        z2_g = sb("z2_g", [P, PACK * S], BF16)
+        z_q = [(sb(f"z_c{h}", [P, W], U32), sb(f"z_s{h}", [P, W], U8)) for h in range(2)]
+        z2_q = (sb("z2_c", [P, S], U32), sb("z2_s", [P, S], U8))
+        w2_q = (sb("w2_c", [P, S], U32), sb("w2_s", [P, S], U8))
+        out_rows = out.rearrange("(p t) n -> p t n", t=PACK)
+        banks_b = [psum.tile([P, S], F32, name=f"bank_b{t}", tag=f"bb{t}") for t in range(PACK)]
 
-        def neigh(t):
-            g1 = sb(f"g1{t}", [P, S], F32)
-            for h in range(2):
-                gather("S", g1[:, W * h : W * (h + 1)], y[t][:], n1_t[:, 16 * h : 16 * (h + 1)])
-            nc.vector.tensor_tensor(big[t][:], g1[:], y[t][:], ALU.max)
+        def clock(name, src):
+            c = sb(name, [P, 1], src.dtype)
+            nc.gpsimd.tensor_copy(out=c[:], in_=src)
+
+        def pa(t, eng="S"):
+            gather(eng, npa[t][:], y[t][:], n2_t[:], -1.0)
+
+        def pbg(t, eng="S"):
+            gather(eng, pb[t][:], y[t][:], n3_t[:])
+
+        def rb_sa(t):
+            nc.vector.scalar_tensor_tensor(rb[t][:], npa[t][:], -0.5, pb[t][:], ALU.mult, ALU.max)
+            nc.vector.tensor_tensor(dt[t][:].indirect(n2_t[:]), pb[t][:], npa[t][:], ALU.add)
+
+        def sbs(t):
+            nc.vector.tensor_copy(dt[t][:].indirect(n3_t[:]), rb[t][:])
+
+        def N(t, h, eng="S"):
+            gather(eng, g1[t][:, W * h : W * (h + 1)], y[t][:], n1_t[:, 16 * h : 16 * (h + 1)])
+
+        def mx(t):
+            nc.vector.tensor_tensor(big[t][:], g1[t][:], y[t][:], ALU.max)
+
+        def weave(eng, dst, planes, c0, c1):
+            o = dst[:, PACK * c0 : PACK * c1].rearrange("p (c i t) -> p c t i", i=4, t=PACK)
+            i = planes[:, :, c0:c1].rearrange("p t (c i) -> p c t i", i=4)
+            if eng == "S":
+                nc.scalar.copy(out=o, in_=i)
+            else:
+                nc.vector.tensor_copy(out=o, in_=i)
+
+        def quant(q, src, c0, c1):
+            nc.vector.quantize_mx(out=q[0][:, c0:c1].bitcast(FP8X4), scales=q[1][:, c0:c1], in_=src[:, PACK * c0 : PACK * c1])
+
+        def Wd(eng, m0, m1):
+            h = m0 // 64
+            order = "p m t j" if eng == "G" else "p m j t"
+            o = w2_g[:].rearrange("p (t m j) -> " + order, t=PACK, j=PACK)[:, m0:m1]
+            i = w2_raw[h][:, :, PACK * (m0 - 64 * h) : PACK * (m1 - 64 * h)].rearrange("p j (m t) -> " + order, t=PACK)
+            if eng == "S":
+                nc.scalar.copy(out=o, in_=i)
+            elif eng == "G":
+                nc.gpsimd.tensor_scalar(o, i, 1.0, 0.0, ALU.mult, ALU.add)
+            else:
+                nc.vector.tensor_copy(out=o, in_=i)
+
+        def mm_b():
+            for t in range(PACK):
+                product(banks_b[t], t, (xc_w, xc_s), z2_q)
+
+        def B(t):
+            nc.scalar.copy(out=b[t][:], in_=banks_b[t][:])
+
+        def quantz(h):
+            nc.vector.quantize_mx(out=z_q[h][0][:].bitcast(FP8X4), scales=z_q[h][1][:], in_=z_g[:, PACK * W * h : PACK * W * (h + 1)])
+
+        def a_pass(bank, t, h):
+            pass_half(bank, t, h, w2_q, z_q[h][0][:], z_q[h][1][:])
+
+        def Ah(h):
+            half = slice(W * h, W * (h + 1))
+            bank = psum.tile([P, S], F32, name=f"bank_a0{h}", tag=f"yb{h}")
+            a_pass(bank, 0, h)
+            nc.scalar.copy(out=a[0][:, half], in_=bank[:, half])
+
+        def A(t):
+            bank = psum.tile([P, S], F32, name=f"bank_a{t}", tag="yb1")
+            a_pass(bank, t, 0)
+            a_pass(bank, t, 1)
+            nc.scalar.copy(out=a[t][:], in_=bank[:])
+
+        def gA(t, eng="S"):
+            gather(eng, ga[t][:], a[t][:], n4_t[:], -0.5)
+
+        def gB(t, eng="S"):
+            gather(eng, gb[t][:], b[t][:], n5_t[:], 0.0625)
+
+        def so(t):
+            nc.vector.tensor_tensor(a[t][:].indirect(n4_t[:]), gb[t][:], ga[t][:], ALU.add)
+            nc.sync.dma_start(out=out_rows[:, t, :], in_=a[t][:])
 
         def cz(t, eng):
             cast(eng, z_planes[:, t, :], big[t][:], gn_t[:, t : t + 1])
@@ -166,57 +258,73 @@ def tile_picked_fkcdputbbiglift_none_p_kernel(tc, x_words, x_scales, w1, gn, w2,
         def cd(t, eng):
             cast(eng, z2_planes[:, t, :], dt[t][:], gs_t[:, t : t + 1])
 
-        pairs(0, "V")
+        pa(0)
+        pbg(0,"V")
+        rb_sa(0)
+        sbs(0)
         evac_y(1)
-        neigh(0)
-        pairs(1)
+        N(0,0)
+        pa(1)
+        pbg(1)
+        rb_sa(1)
+        N(0,1)
+        mx(0)
+        sbs(1)
         evac_y(2)
-        neigh(1)
+        N(1,0)
+        pa(2)
+        pbg(2)
+        rb_sa(2)
+        N(1,1)
+        mx(1)
+        sbs(2)
+        cd(0,"S")
+        cz(0,"S")
         evac_y(3)
-        neigh(2)
-        pairs(2)
-        neigh(3)
-        cz(3, "V")
-        cz(0, "S")
-        cz(1, "S")
-        cz(2, "S")
-        z_q = quantize("z", interleave("z_g", z_planes))
-        for h in range(2):
-            deal_weight(w2_g, w2_raw[:, :, W * h : W * (h + 1)], 64 * h, 64 * (h + 1))
-        w2_q = quantize("w2", w2_g)
-        banks_a = [psum.tile([P, S], F32, name=f"bank_a{t}", tag=f"ab{t}") for t in range(PACK)]
-        for t in range(PACK):
-            product(banks_a[t], t, w2_q, z_q)
-        pairs(3)
-        cd(3, "V")
-        for t in range(3):
-            cd(t, "S")
-        z2_g = interleave("z2_g", z2_planes)
-        z2_c = sb("z2_c", [P, S], U32)
-        z2_s = sb("z2_s", [P, S], U8)
-        for h in range(2):
-            half = slice(W * h, W * (h + 1))
-            nc.vector.quantize_mx(out=z2_c[:, half].bitcast(FP8X4), scales=z2_s[:, half], in_=z2_g[:, 4 * W * h : 4 * W * (h + 1)])
-        a = [sb(f"a{t}", [P, S], F32) for t in range(PACK)]
-        ga = [sb(f"ga{t}", [P, W], F32) for t in range(PACK)]
-        for t in range(PACK):
-            nc.scalar.copy(out=a[t][:], in_=banks_a[t][:])
-        for t in range(PACK):
-            gather("S" if t < 2 else "V", ga[t][:], a[t][:], n4_t[:], -0.5)
-
-        out_rows = out.rearrange("(p t) n -> p t n", t=PACK)
-        banks_b = [psum.tile([P, S], F32, name=f"bank_b{t}", tag=f"yb{t}") for t in range(PACK)]
-        b = [sb(f"b{t}", [P, S], F32) for t in range(PACK)]
-        for h in range(2):
-            half = slice(W * h, W * (h + 1))
-            product_half(banks_b[0], 0, h, (xc_w, xc_s), (z2_c, z2_s))
-            nc.scalar.copy(out=b[0][:, half], in_=banks_b[0][:, half])
-        for t in range(1, PACK):
-            product(banks_b[t], t, (xc_w, xc_s), (z2_c, z2_s))
-        for t in range(PACK):
-            if t > 0:
-                nc.scalar.copy(out=b[t][:], in_=banks_b[t][:])
-            gb = sb(f"gb{t}", [P, W], F32)
-            gather("S", gb[:], b[t][:], n5_t[:], 0.0625)
-            nc.vector.tensor_tensor(a[t][:].indirect(n4_t[:]), gb[:], ga[t][:], ALU.add)
-            nc.sync.dma_start(out=out_rows[:, t, :], in_=a[t][:])
+        N(2,0)
+        pa(3)
+        pbg(3)
+        rb_sa(3)
+        N(2,1)
+        mx(2)
+        sbs(3)
+        cd(1,"S")
+        cz(1,"S")
+        N(3,0)
+        N(3,1)
+        mx(3)
+        cd(2,"S")
+        Wd("S",0,64)
+        cz(2,"S")
+        cd(3,"S")
+        weave("V",z2_g,z2_planes,0,512)
+        quant(z2_q,z2_g,0,512)
+        mm_b()
+        cz(3,"S")
+        weave("V",z_g,z_planes,0,256)
+        Wd("S",64,128)
+        quant(w2_q,w2_g,0,512)
+        weave("S",z_g,z_planes,256,512)
+        quantz(0)
+        quantz(1)
+        B(0)
+        gB(0,"V")
+        B(1)
+        gB(1,"V")
+        B(2)
+        gB(2,"V")
+        Ah(0)
+        Ah(1)
+        B(3)
+        gB(3,"V")
+        gA(0)
+        so(0)
+        A(1)
+        gA(1)
+        so(1)
+        A(2)
+        gA(2)
+        so(2)
+        A(3)
+        gA(3)
+        so(3)

@@ -45,7 +45,7 @@ def tile_picked_fkcdputbbiglift_none_p_kernel(tc, x_words, x_scales, w1, gn, w2,
         w1_raw = [sb(f"w1_raw{h}", [P, PACK, W], F32) for h in range(2)]
         nc.sync.dma_start(out=w1_raw[0][:], in_=w1_rows[:, :, 0:W])
         for q in range(4):
-            nc.sync.dma_start(out=xs[32 * q : 32 * q + 4, :].bitcast(I32), in_=x_scales[0, 4 * q : 4 * q + 4, :].bitcast(I32))
+            nc.sync.dma_start(out=xs[q:P:32, :].bitcast(I32), in_=x_scales[0, q:16:4, :].bitcast(I32))
         cand_t = load_list("cand_t", cand)
         nc.sync.dma_start(out=w1_raw[1][:], in_=w1_rows[:, :, W:S])
         xw = sb("xw", [P, T], I32)

from contextlib import ExitStack

import concourse.mybir as mybir

F32 = mybir.dt.float32
BF16 = mybir.dt.bfloat16
I32 = mybir.dt.int32
U32 = mybir.dt.uint32
U16 = mybir.dt.uint16
U8 = mybir.dt.uint8
FP8X4 = mybir.dt.float8_e4m3fn_x4
ALU = mybir.AluOpType
COPY = mybir.ActivationFunctionType.Copy

P = 128
PACK = 4
T = 2048
S = 512
W = 256
FLOPS = 3 * 2 * 512 * 512 * 512


def tile_picked_fkcdputbbiglift_none_p_kernel(tc, x_words, x_scales, w1, gn, w2, gs, offs, n1, n2, n3, cand, n4, n5, out):
    nc = tc.nc
    with ExitStack() as ctx:
        keep = ctx.enter_context(tc.tile_pool(name="keep", bufs=1))
        psum = ctx.enter_context(tc.psum_pool(name="psum", bufs=1))

        def sb(name, shape, dtype):
            return keep.tile(shape, dtype, name=name, align_bytes=64)

        def load_list(name, src):
            tile = sb(name, list(src.shape), U16)
            nc.sync.dma_start(out=tile[:], in_=src)
            return tile


        xs = sb("xs", [P, T], U8)
        nc.vector.memset(xs[:].bitcast(I32), 0)
        gn_t = sb("gn_t", [P, PACK], F32)
        gs_t = sb("gs_t", [P, PACK], F32)
        w1_rows = w1.rearrange("(p j) c -> p j c", j=PACK)
        w2_rows = w2.rearrange("(p j) c -> p j c", j=PACK)
        offs_t = load_list("offs_t", offs)
        w1_raw = [sb(f"w1_raw{h}", [P, PACK, W], F32) for h in range(2)]
        nc.sync.dma_start(out=w1_raw[0][:], in_=w1_rows[:, :, 0:W])
        for q in range(4):
            nc.sync.dma_start(out=xs[q:P:32, :].bitcast(I32), in_=x_scales[0, q:16:4, :].bitcast(I32))
        cand_t = load_list("cand_t", cand)
        nc.sync.dma_start(out=w1_raw[1][:], in_=w1_rows[:, :, W:S])
        xw = sb("xw", [P, T], I32)
        nc.sync.dma_start(out=xw[:], in_=x_words[0].rearrange("p n r -> p (n r)").bitcast(I32))
        n2_t = load_list("n2_t", n2)
        n3_t = load_list("n3_t", n3)
        w2_raw = [sb(f"w2_raw{h}", [P, PACK, W], F32) for h in range(2)]
        for h in range(2):
            nc.sync.dma_start(out=w2_raw[h][:], in_=w2_rows[:, :, W * h : W * (h + 1)])
        n1_t = load_list("n1_t", n1)
        nc.sync.dma_start(out=gn_t[:], in_=gn.rearrange("(p t) o -> p (t o)", t=PACK))
        nc.sync.dma_start(out=gs_t[:], in_=gs.rearrange("(p t) o -> p (t o)", t=PACK))
        n4_t = load_list("n4_t", n4)
        n5_t = load_list("n5_t", n5)

        def deal_weight(dst, raw, m0, m1):
            nc.scalar.copy(
                out=dst[:].rearrange("p (t m j) -> p m j t", t=PACK, j=PACK)[:, m0:m1],
                in_=raw.rearrange("p j (m t) -> p m j t", t=PACK),
            )

        def quantize(name, src):
            codes = sb(name + "_c", [P, S], U32)
            scales = sb(name + "_s", [P, S], U8)
            nc.vector.quantize_mx(out=codes[:].bitcast(FP8X4), scales=scales[:], in_=src[:])
            return codes, scales

        def product(bank, t, left, right):
            cols = slice(P * t, P * (t + 1))
            nc.tensor.matmul_mx(out=bank[:], lhsT=left[0][:, cols].bitcast(FP8X4), lhsT_scale=left[1][:, cols],
                                rhs=right[0][:].bitcast(FP8X4), rhs_scale=right[1][:], start=True, stop=True)

        def interleave(name, planes):
            dst = sb(name, [P, PACK * S], BF16)
            nc.vector.tensor_copy(
                out=dst[:].rearrange("p (c i t) -> p c t i", i=4, t=PACK),
                in_=planes[:].rearrange("p t (c i) -> p c t i", i=4),
            )
            return dst


        def product_half(bank, t, h, left, right):
            cols = slice(P * t, P * (t + 1))
            half = slice(W * h, W * (h + 1))
            nc.tensor.matmul_mx(out=bank[:, half], lhsT=left[0][:, cols].bitcast(FP8X4), lhsT_scale=left[1][:, cols],
                                rhs=right[0][:, half].bitcast(FP8X4), rhs_scale=right[1][:, half], start=True, stop=True)

        def gather(eng, dst, window, lst, scale=1.0):
            if eng == "S":
                nc.scalar.activation(dst, window.indirect(lst), COPY, scale=scale)
            elif scale == 1.0:
                nc.vector.tensor_copy(dst, window.indirect(lst))
            else:
                nc.vector.tensor_scalar(dst, window.indirect(lst), scale, 0.0, ALU.mult, ALU.add)

        def cast(eng, dst, src, col):
            if eng == "S":
                nc.scalar.activation(dst, src, COPY, scale=col)
            elif eng == "G":
                nc.gpsimd.tensor_scalar(dst, src, col, 0.0, ALU.mult, ALU.add)
            else:
                nc.vector.tensor_scalar(dst, src, col, None, ALU.mult)

        w1_g = sb("w1_g", [P, PACK * S], BF16)
        deal_weight(w1_g, w1_raw[0][:], 0, 64)
        deal_weight(w1_g, w1_raw[1][:], 64, 128)

        xq_s = sb("xq_s", [P, S], U8)
        nc.vector.tensor_copy(out=xq_s[:], in_=xs[:].indirect(offs_t[:]))
        xc_s0 = sb("xc_s0", [P, S], U8)
        nc.vector.tensor_copy(out=xc_s0[:], in_=xs[:].indirect(cand_t[:]))
        xc_s = sb("xc_s", [P, S], U8)
        nc.vector.tensor_copy(out=xc_s[:].rearrange("p (t m) -> p m t", t=PACK), in_=xc_s0[:].rearrange("p (m t) -> p m t", t=PACK))
        w1_q = quantize("w1", w1_g)
        xq_w = [sb(f"xq_w{h}", [P, W], U32) for h in range(2)]
        y = [sb(f"y{t}", [P, S], F32) for t in range(PACK)]

        def pass_half(bank, t, h, left, codes, scales):
            cols = slice(P * t, P * (t + 1))
            nc.tensor.matmul_mx(out=bank[:, W * h : W * (h + 1)], lhsT=left[0][:, cols].bitcast(FP8X4), lhsT_scale=left[1][:, cols],
                                rhs=codes.bitcast(FP8X4), rhs_scale=scales, start=True, stop=True)

        def y_pass(bank, t, h):
            pass_half(bank, t, h, w1_q, xq_w[h][:], xq_s[:, W * h : W * (h + 1)])

        for h in range(2):
            half = slice(W * h, W * (h + 1))
            nc.vector.tensor_copy(out=xq_w[h][:], in_=xw[:].bitcast(U32).indirect(offs_t[:, 16 * h : 16 * (h + 1)]))
            bank = psum.tile([P, S], F32, name=f"bank_y0{h}", tag=f"yb{h}")
            y_pass(bank, 0, h)
            nc.scalar.copy(out=y[0][:, half], in_=bank[:, half])

        xc_w0 = sb("xc_w0", [P, S], U32)
        nc.vector.tensor_copy(out=xc_w0[:], in_=xw[:].bitcast(U32).indirect(cand_t[:]))
        xc_w = sb("xc_w", [P, S], U32)
        nc.vector.tensor_copy(out=xc_w[:].bitcast(I32).rearrange("p (t m) -> p m t", t=PACK), in_=xc_w0[:].bitcast(I32).rearrange("p (m t) -> p m t", t=PACK))

        z_planes = sb("z_planes", [P, PACK, S], BF16)
        z2_planes = sb("z2_planes", [P, PACK, S], BF16)
        w2_g = sb("w2_g", [P, PACK * S], BF16)
        dt = [sb(f"dt{t}", [P, S], F32) for t in range(PACK)]
        big = [sb(f"big{t}", [P, S], F32) for t in range(PACK)]

        def evac_y(t):
            bank = psum.tile([P, S], F32, name=f"bank_y{t}", tag="yb1")
            y_pass(bank, t, 0)
            y_pass(bank, t, 1)
            nc.scalar.copy(out=y[t][:], in_=bank[:])

        npa = [sb(f"npa{t}", [P, W], F32) for t in range(PACK)]
        pb = [sb(f"pb{t}", [P, W], F32) for t in range(PACK)]
        rb = [sb(f"rb{t}", [P, W], F32) for t in range(PACK)]
        g1 = [sb(f"g1{t}", [P, S], F32) for t in range(PACK)]
        a = [sb(f"a{t}", [P, S], F32) for t in range(PACK)]
        b = [sb(f"b{t}", [P, S], F32) for t in range(PACK)]
        ga = [sb(f"ga{t}", [P, W], F32) for t in range(PACK)]
        gb = [sb(f"gb{t}", [P, W], F32) for t in range(PACK)]
        z_g = sb("z_g", [P, PACK * S], BF16)
        z2_g = sb("z2_g", [P, PACK * S], BF16)
        z_q = [(sb(f"z_c{h}", [P, W], U32), sb(f"z_s{h}", [P, W], U8)) for h in range(2)]
        z2_q = (sb("z2_c", [P, S], U32), sb("z2_s", [P, S], U8))
        w2_q = (sb("w2_c", [P, S], U32), sb("w2_s", [P, S], U8))
        out_rows = out.rearrange("(p t) n -> p t n", t=PACK)
        banks_b = [psum.tile([P, S], F32, name=f"bank_b{t}", tag=f"bb{t}") for t in range(PACK)]

        def clock(name, src):
            c = sb(name, [P, 1], src.dtype)
            nc.gpsimd.tensor_copy(out=c[:], in_=src)

        def pa(t, eng="S"):
            gather(eng, npa[t][:], y[t][:], n2_t[:], -1.0)

        def pbg(t, eng="S"):
            gather(eng, pb[t][:], y[t][:], n3_t[:])

        def rb_sa(t):
            nc.vector.scalar_tensor_tensor(rb[t][:], npa[t][:], -0.5, pb[t][:], ALU.mult, ALU.max)
            nc.vector.tensor_tensor(dt[t][:].indirect(n2_t[:]), pb[t][:], npa[t][:], ALU.add)

        def sbs(t):
            nc.vector.tensor_copy(dt[t][:].indirect(n3_t[:]), rb[t][:])

        def N(t, h, eng="S"):
            gather(eng, g1[t][:, W * h : W * (h + 1)], y[t][:], n1_t[:, 16 * h : 16 * (h + 1)])

        def mx(t):
            nc.vector.tensor_tensor(big[t][:], g1[t][:], y[t][:], ALU.max)

        def weave(eng, dst, planes, c0, c1):
            o = dst[:, PACK * c0 : PACK * c1].rearrange("p (c i t) -> p c t i", i=4, t=PACK)
            i = planes[:, :, c0:c1].rearrange("p t (c i) -> p c t i", i=4)
            if eng == "S":
                nc.scalar.copy(out=o, in_=i)
            else:
                nc.vector.tensor_copy(out=o, in_=i)

        def quant(q, src, c0, c1):
            nc.vector.quantize_mx(out=q[0][:, c0:c1].bitcast(FP8X4), scales=q[1][:, c0:c1], in_=src[:, PACK * c0 : PACK * c1])

        def Wd(eng, m0, m1):
            h = m0 // 64
            order = "p m t j" if eng == "G" else "p m j t"
            o = w2_g[:].rearrange("p (t m j) -> " + order, t=PACK, j=PACK)[:, m0:m1]
            i = w2_raw[h][:, :, PACK * (m0 - 64 * h) : PACK * (m1 - 64 * h)].rearrange("p j (m t) -> " + order, t=PACK)
            if eng == "S":
                nc.scalar.copy(out=o, in_=i)
            elif eng == "G":
                nc.gpsimd.tensor_scalar(o, i, 1.0, 0.0, ALU.mult, ALU.add)
            else:
                nc.vector.tensor_copy(out=o, in_=i)

        def mm_b():
            for t in range(PACK):
                product(banks_b[t], t, (xc_w, xc_s), z2_q)

        def B(t):
            nc.scalar.copy(out=b[t][:], in_=banks_b[t][:])

        def quantz(h):
            nc.vector.quantize_mx(out=z_q[h][0][:].bitcast(FP8X4), scales=z_q[h][1][:], in_=z_g[:, PACK * W * h : PACK * W * (h + 1)])

        def a_pass(bank, t, h):
            pass_half(bank, t, h, w2_q, z_q[h][0][:], z_q[h][1][:])

        def Ah(h):
            half = slice(W * h, W * (h + 1))
            bank = psum.tile([P, S], F32, name=f"bank_a0{h}", tag=f"yb{h}")
            a_pass(bank, 0, h)
            nc.scalar.copy(out=a[0][:, half], in_=bank[:, half])

        def A(t):
            bank = psum.tile([P, S], F32, name=f"bank_a{t}", tag="yb1")
            a_pass(bank, t, 0)
            a_pass(bank, t, 1)
            nc.scalar.copy(out=a[t][:], in_=bank[:])

        def gA(t, eng="S"):
            gather(eng, ga[t][:], a[t][:], n4_t[:], -0.5)

        def gB(t, eng="S"):
            gather(eng, gb[t][:], b[t][:], n5_t[:], 0.0625)

        def so(t):
            nc.vector.tensor_tensor(a[t][:].indirect(n4_t[:]), gb[t][:], ga[t][:], ALU.add)
            nc.sync.dma_start(out=out_rows[:, t, :], in_=a[t][:])

        def cz(t, eng):
            cast(eng, z_planes[:, t, :], big[t][:], gn_t[:, t : t + 1])

        def cd(t, eng):
            cast(eng, z2_planes[:, t, :], dt[t][:], gs_t[:, t : t + 1])

        pa(0)
        pbg(0,"V")
        rb_sa(0)
        sbs(0)
        evac_y(1)
        N(0,0)
        pa(1)
        pbg(1)
        rb_sa(1)
        N(0,1)
        mx(0)
        sbs(1)
        evac_y(2)
        N(1,0)
        pa(2)
        pbg(2)
        rb_sa(2)
        N(1,1)
        mx(1)
        sbs(2)
        cd(0,"S")
        cz(0,"S")
        evac_y(3)
        N(2,0)
        pa(3)
        pbg(3)
        rb_sa(3)
        N(2,1)
        mx(2)
        sbs(3)
        cd(1,"S")
        cz(1,"S")
        N(3,0)
        N(3,1)
        mx(3)
        cd(2,"S")
        Wd("S",0,64)
        cz(2,"S")
        cd(3,"S")
        weave("V",z2_g,z2_planes,0,512)
        quant(z2_q,z2_g,0,512)
        mm_b()
        cz(3,"S")
        weave("V",z_g,z_planes,0,256)
        Wd("S",64,128)
        quant(w2_q,w2_g,0,512)
        weave("S",z_g,z_planes,256,512)
        quantz(0)
        quantz(1)
        B(0)
        gB(0,"V")
        B(1)
        gB(1,"V")
        B(2)
        gB(2,"V")
        Ah(0)
        Ah(1)
        B(3)
        gB(3,"V")
        gA(0)
        so(0)
        A(1)
        gA(1)
        so(1)
        A(2)
        gA(2)
        so(2)
        A(3)
        gA(3)
        so(3)
